import numpy as np
import ml_dtypes


def mxq(x, axis, fmt="e4m3"):
    dtype, down = {"e4m3": (ml_dtypes.float8_e4m3fn, 7), "e5m2": (ml_dtypes.float8_e5m2, 14)}[fmt]
    v = np.moveaxis(np.asarray(x, np.float32).astype(ml_dtypes.bfloat16).astype(np.float64), axis, -1)
    blocks = v.reshape(v.shape[:-1] + (-1, 32))
    amax = np.abs(blocks).max(-1, keepdims=True)
    byte = np.maximum(np.where(amax > 0, np.frexp(amax)[1] - 1 + 127, 0) - down, 1)
    scale = np.exp2(byte - 127.0)
    codes = (blocks / scale).astype(np.float32).astype(dtype).astype(np.float64)
    return np.moveaxis((codes * scale).reshape(v.shape), -1, axis)


WIDE = False


def mx_kscale(k):
    if not WIDE:
        return np.ones(k)
    levels = np.array([10, -10, 5, -5, 0])
    if k % 512:
        return np.exp2(np.random.permutation(np.resize(levels, k // 32))).repeat(32)
    a = np.empty((k // 512, 16))
    for p in range(k // 512):
        a[p, :8] = np.random.permutation(np.resize(levels, 8))
        for g in range(8):
            far = levels[np.abs(levels - a[p, g]) >= 10]
            a[p, g + 8] = far[np.random.randint(len(far))]
    return np.exp2(a.ravel()).repeat(32)


def f64(x):
    return np.asarray(x).astype(np.float64)


def striped(idx):
    return np.tile(idx.reshape(-1, 16).T, (8, 1)).astype(np.uint16)


def unstriped(offs):
    return offs[:16].T.reshape(-1).astype(np.int64)


def pack_weight(w):
    k, n = w.shape
    w = f64(np.asarray(w, np.float32).astype(ml_dtypes.bfloat16)).reshape(k // 32, 32, n)
    amax = np.abs(w).max(1)
    byte = np.clip(np.where(amax > 0, np.frexp(amax)[1] - 1 + 127 - 7, 1), 1, 254)
    scaled = (w * np.exp2(127.0 - byte)[:, None, :]).reshape(k, n).astype(np.float32)
    words = np.ascontiguousarray(scaled.reshape(k // 512, 128, 4, n).transpose(0, 1, 3, 2)).astype(ml_dtypes.float8_e4m3fn).view(np.uint8)
    return words, np.ascontiguousarray(byte.astype(np.uint8).reshape(k // 512, 16, n))


def unpack_weight(words, scales):
    g, p, n, _ = words.shape
    vals = np.ascontiguousarray(words).view(ml_dtypes.float8_e4m3fn).astype(np.float64) * np.repeat(np.exp2(scales.astype(np.float64) - 127.0), 8, axis=1)[..., None]
    return vals.transpose(0, 1, 3, 2).reshape(g * 512, n)


def planes(y):
    n, m = y.shape
    v = y.astype(np.float32).astype(ml_dtypes.bfloat16).astype(np.float64).reshape(n // 32, 32, m)
    top = np.abs(v).max(1)
    byte = np.clip(np.where(top > 0, np.frexp(top)[1] - 1 + 127 - 7, 1), 1, 254)
    codes = (v * np.exp2(127.0 - byte)[:, None, :]).reshape(n, m).astype(np.float32).astype(ml_dtypes.float8_e4m3fn).view(np.uint8)
    words = codes.reshape(n // 512, 128, 4, m).transpose(0, 1, 3, 2)
    return np.ascontiguousarray(words), np.ascontiguousarray(byte.astype(np.uint8).reshape(n // 512, 16, m))


def sigmoid(v):
    return 1.0 / (1.0 + np.exp(-np.maximum(v, -700.0)))


K, T, S, N, H, W, G, U = 512, 1024, 512, 512, 512, 1024, 1024, 1024


def setup_inputs():
    n = np.random.standard_normal
    s = mx_kscale(K)[:, None]
    u = mx_kscale(H)
    packed_xT = pack_weight(n((K, T)) * s)
    packed_eT = pack_weight(n((K, W)) * s)
    packed_dT = pack_weight(n((K, G)) * s)
    return {
        "x_words": packed_xT[0],
        "x_scales": packed_xT[1],
        "w1": (n((K, N)) / np.sqrt(K) / s).astype(np.float32),
        "e_words": packed_eT[0],
        "e_scales": packed_eT[1],
        "w2": (n((K, N)) / np.sqrt(K) / s).astype(np.float32),
        "d_words": packed_dT[0],
        "d_scales": packed_dT[1],
        "w3": (n((K, N)) / np.sqrt(K) / s).astype(np.float32),
        "unit": (np.random.uniform(0.6, 1.4, (H, 1)) * u[:, None]).astype(np.float32),
        "w4": (n((H, N)) / np.sqrt(H) / u[:, None]).astype(np.float32),
        "offs": striped(np.random.permutation(T)[:S]),
        "ton": striped(np.random.permutation(W)[:S]),
        "sty": striped(np.random.permutation(G)[:S]),
        "ph": striped(np.random.permutation(np.concatenate([np.arange(S), np.random.randint(0, S, U - S)]))),
        "tn": striped(np.random.permutation(np.concatenate([np.arange(S), np.random.randint(0, S, U - S)]))),
        "mix_": striped(np.random.permutation(S)),
        "sp1": striped(np.random.permutation(np.concatenate([np.arange(S), np.random.randint(0, S, U - S)]))),
    }


def reference(x_words, x_scales, w1, e_words, e_scales, w2, d_words, d_scales, w3, unit, w4, offs, ton, sty, ph, tn, mix_, sp1):
    xq = unpack_weight(x_words, x_scales)[:, unstriped(offs)]
    y = mxq(f64(w1), 0, "e4m3").T @ xq
    yp = y[:, unstriped(ph)]
    d_sty = unpack_weight(d_words, d_scales)[:, unstriped(sty)]
    yd = mxq(f64(w3), 0, "e4m3").T @ d_sty
    dm = yd[:, unstriped(mix_)]
    style = yd + 0.5 * dm
    ys1 = style[:, unstriped(sp1)]
    frm = yp * (np.tanh(ys1) + 1.0)
    e_ton = unpack_weight(e_words, e_scales)[:, unstriped(ton)]
    ye = mxq(f64(w2), 0, "e4m3").T @ e_ton
    et1 = ye[:, unstriped(tn)]
    hid = f64(unit) * (frm * sigmoid(et1))
    out_0 = mxq(f64(w4), 0, "e4m3").T @ mxq(hid, 0, "e4m3")
    return (out_0,) + planes(out_0)

@@ -1,0 +1,235 @@
+from contextlib import ExitStack
+
+import concourse.mybir as mybir
+
+K, T, S, H, N, U = 512, 1024, 512, 512, 512, 1024
+FLOPS = 2 * K * H * S * 3 + 2 * H * N * U
+
+F32 = mybir.dt.float32
+BF16 = mybir.dt.bfloat16
+I32 = mybir.dt.int32
+U32 = mybir.dt.uint32
+U16 = mybir.dt.uint16
+U8 = mybir.dt.uint8
+FP8X4 = mybir.dt.float8_e4m3fn_x4
+MULT = mybir.AluOpType.mult
+ADD = mybir.AluOpType.add
+COPY = mybir.ActivationFunctionType.Copy
+SIGMOID = mybir.ActivationFunctionType.Sigmoid
+
+P = 128
+PACK = 4
+LIST = 16
+SPARE = 16
+BANK = 512
+CHUNKS = (512, 256, 256)
+
+
+def tile_picked_yttsfrm_gate_po_kernel(
+    tc, x_words, x_scales, w1, e_words, e_scales, w2, d_words, d_scales, w3, unit, w4,
+    offs, ton, sty, ph, tn, mix_, sp1, out_0, out_1, out_2,
+):
+    nc = tc.nc
+    with ExitStack() as ctx:
+        keep = ctx.enter_context(tc.tile_pool(name="keep", bufs=1))
+        psum = ctx.enter_context(tc.psum_pool(name="psum", bufs=1))
+
+        def sb(name, shape, dtype):
+            return keep.tile(shape, dtype, name=name, align_bytes=64)
+
+        def bank(b):
+            return psum.tile([P, BANK], F32, name="bank%d" % b)
+
+        def load_list(name, src):
+            t = sb(name, list(src.shape), U16)
+            nc.sync.dma_start(t[:], src)
+            return t
+
+        def load_words(name, words):
+            t = sb(name + "_words", [P, T], U32)
+            nc.sync.dma_start(t[:].bitcast(I32), words[0].rearrange("p n r -> p (n r)").bitcast(I32))
+            return t
+
+        def load_scales(name, scales, queue):
+            t = sb(name + "_scales", [P, T], U8)
+            nc.gpsimd.memset(t[:].bitcast(I32), 0)
+            for q in range(4):
+                queue.dma_start(t[32 * q : 32 * q + 4, :].bitcast(I32), scales[0, 4 * q : 4 * q + 4, :].bitcast(I32))
+            return t
+
+        def load_weight(name, w, parts):
+            width = w.shape[1] // parts
+            raws = []
+            for h in range(parts):
+                raw = sb("%s_raw%d" % (name, h), [P, PACK, width], F32)
+                nc.sync.dma_start(raw[:], w[:, h * width : (h + 1) * width].rearrange("(p j) c -> p j c", j=PACK))
+                raws.append(raw)
+            return raws
+
+        def pick(name, words, scales, offsets):
+            picked_scales = sb(name + "_picked_scales", [P, S], U8)
+            picked_words = sb(name + "_picked_words", [P, S], U32)
+            nc.vector.tensor_copy(picked_words[:], words[:].indirect(offsets[:]))
+            nc.vector.tensor_copy(picked_scales[:], scales[:].indirect(offsets[:]))
+            return picked_words, picked_scales
+
+        def quantise(name, grouped, width):
+            codes = sb(name + "_codes", [P, width], U32)
+            scales = sb(name + "_qscales", [P, width], U8)
+            nc.vector.quantize_mx(out=codes[:].bitcast(FP8X4), scales=scales[:], in_=grouped)
+            return codes, scales
+
+        def quantise_weight(name, raws, copies):
+            grouped = sb(name + "_bf16", [P, PACK, P, PACK], BF16)
+            m = P // len(raws)
+            for h in range(len(raws)):
+                copies[h](
+                    grouped[:, :, h * m : (h + 1) * m, :].rearrange("p t m j -> p m j t"),
+                    raws[h][:].rearrange("p j (m t) -> p m j t", t=PACK),
+                )
+            return quantise(name, grouped[:].rearrange("p t m j -> p (t m j)"), PACK * P)
+
+        def product(out, weight, t, moving):
+            cols = slice(t * P, (t + 1) * P)
+            nc.tensor.matmul_mx(
+                out=out, lhsT=weight[0][:, cols].bitcast(FP8X4), lhsT_scale=weight[1][:, cols],
+                rhs=moving[0][:].bitcast(FP8X4), rhs_scale=moving[1][:], start=True, stop=True,
+            )
+
+        def window(name):
+            t = sb(name, [P, S + SPARE], F32)
+            nc.gpsimd.memset(t[:, S:], 0.0)
+            return t
+
+        d_scale_table = load_scales("d", d_scales, nc.scalar)
+        sty_l = load_list("sty_l", sty)
+        d_word_table = load_words("d", d_words)
+        w3_raw = load_weight("w3", w3, 2)
+        x_scale_table = load_scales("x", x_scales, nc.gpsimd)
+        e_scale_table = load_scales("e", e_scales, nc.gpsimd)
+        offs_l = load_list("offs_l", offs)
+        x_word_table = load_words("x", x_words)
+        mix_l = load_list("mix_l", mix_)
+        w1_raw = load_weight("w1", w1, 1)
+        sp1_l = load_list("sp1_l", sp1)
+        unit_t = sb("unit_t", [P, PACK], F32)
+        nc.sync.dma_start(unit_t[:], unit.rearrange("(p t) o -> p (t o)", t=PACK))
+        ton_l = load_list("ton_l", ton)
+        e_word_table = load_words("e", e_words)
+        w2_raw = load_weight("w2", w2, 1)
+        ph_l = load_list("ph_l", ph)
+        tn_l = load_list("tn_l", tn)
+        w4_raw = load_weight("w4", w4, 1)
+
+        yd = [window("yd%d" % t) for t in range(PACK)]
+        phoneme = [window("phoneme%d" % t) for t in range(PACK)]
+        tone = [window("tone%d" % t) for t in range(PACK)]
+        style2 = [sb("style2_%d" % t, [P, 2 * S], F32) for t in range(PACK)]
+
+        d_picked = pick("d", d_word_table, d_scale_table, sty_l)
+        w3_q = quantise_weight("w3", w3_raw, (nc.scalar.copy, nc.vector.tensor_copy))
+        yd_banks = [bank(t) for t in range(PACK)]
+        for t in range(PACK):
+            product(yd_banks[t][:], w3_q, t, d_picked)
+        for t in range(PACK):
+            nc.scalar.copy(yd[t][:, :S], yd_banks[t][:])
+            nc.scalar.activation(style2[t][:, S:], yd[t][:].indirect(mix_l[:]), COPY)
+
+        x_picked = pick("x", x_word_table, x_scale_table, offs_l)
+        w1_q = quantise_weight("w1", w1_raw, (nc.vector.tensor_copy,))
+        unit2 = sb("unit2", [P, PACK], F32)
+        nc.vector.tensor_scalar(unit2[:], unit_t[:], 2.0, None, MULT)
+        for t in range(PACK):
+            nc.vector.scalar_tensor_tensor(style2[t][:, :S], yd_banks[t][:], 2.0, style2[t][:, S:], MULT, ADD)
+        for t in range(PACK):
+            y_bank = bank(PACK + t)
+            product(y_bank[:], w1_q, t, x_picked)
+            nc.scalar.activation(phoneme[t][:, :S], y_bank[:], COPY, scale=unit2[:, t : t + 1])
+
+        e_picked = pick("e", e_word_table, e_scale_table, ton_l)
+        w2_q = quantise_weight("w2", w2_raw, (nc.vector.tensor_copy,))
+
+        starts = [sum(CHUNKS[:c]) for c in range(len(CHUNKS))]
+
+        def piece(offsets, c):
+            return offsets[:, starts[c] // LIST : (starts[c] + CHUNKS[c]) // LIST]
+
+        def look_up_styles(c):
+            bounded = sb("bounded%d" % c, [P, PACK, CHUNKS[c]], F32)
+            for t in range(PACK):
+                nc.scalar.activation(bounded[:, t, :], style2[t][:].indirect(piece(sp1_l, c)), SIGMOID)
+            return bounded
+
+        def frames(c, bounded):
+            frm = sb("frm%d" % c, [P, PACK, CHUNKS[c]], F32)
+            for t in range(PACK):
+                nc.vector.tensor_tensor(frm[:, t, :], phoneme[t][:].indirect(piece(ph_l, c)), bounded[:, t, :], MULT)
+            return frm
+
+        def look_up_tones(c):
+            gate = sb("gate%d" % c, [P, PACK, CHUNKS[c]], F32)
+            for t in range(PACK):
+                nc.scalar.activation(gate[:, t, :], tone[t][:].indirect(piece(tn_l, c)), COPY)
+            return gate
+
+        def by_fours(grouped, planes):
+            return (
+                grouped[:].rearrange("p (c i) t -> p c t i", i=4),
+                [a[:].rearrange("p t (c i) -> p c t i", i=4) for a in planes],
+            )
+
+        def hidden(c, frm, gate):
+            hid = sb("hid%d" % c, [P, CHUNKS[c], PACK], BF16)
+            dst, (a, b) = by_fours(hid, (frm, gate))
+            nc.vector.tensor_tensor(dst, a, b, MULT)
+            return quantise("hid%d" % c, hid[:].rearrange("p n t -> p (n t)"), CHUNKS[c])
+
+        out_scales = sb("out_scales", [P, U], U8)
+        out_rows = out_0.rearrange("(p t) r -> p t r", t=PACK)
+        out_words = out_1[0].rearrange("p n r -> p (n r)").bitcast(I32)
+
+        def bands(c, hid_q, first_bank):
+            n = CHUNKS[c]
+            cols = slice(starts[c], starts[c] + n)
+            per_bank = BANK // n
+            result = sb("result%d" % c, [P, PACK, n], F32)
+            for b in range(PACK // per_bank):
+                acc = bank(first_bank + b)
+                for s in range(per_bank):
+                    product(acc[:, s * n : (s + 1) * n], w4_q, b * per_bank + s, hid_q)
+                ts = slice(b * per_bank, (b + 1) * per_bank)
+                nc.scalar.copy(result[:, ts, :].rearrange("p t n -> p (t n)"), acc[:])
+            nc.sync.dma_start(out_rows[:, :, cols], result[:])
+            rounded = sb("rounded%d" % c, [P, n, PACK], BF16)
+            dst, (src,) = by_fours(rounded, (result,))
+            nc.vector.tensor_copy(dst, src)
+            codes = sb("out_codes%d" % c, [P, n], U32)
+            nc.vector.quantize_mx(
+                out=codes[:].bitcast(FP8X4), scales=out_scales[:, cols], in_=rounded[:].rearrange("p n t -> p (n t)")
+            )
+            nc.sync.dma_start(out_words[:, cols], codes[:].bitcast(I32))
+
+        bounded0 = look_up_styles(0)
+        for t in range(PACK):
+            ye_bank = bank(t)
+            product(ye_bank[:], w2_q, t, e_picked)
+            nc.scalar.activation(tone[t][:, :S], ye_bank[:], SIGMOID)
+        w4_q = quantise_weight("w4", w4_raw, (nc.vector.tensor_copy,))
+        frm0 = frames(0, bounded0)
+        gate0 = look_up_tones(0)
+        bounded1 = look_up_styles(1)
+        hid0 = hidden(0, frm0, gate0)
+        frm1 = frames(1, bounded1)
+        gate1 = look_up_tones(1)
+        bounded2 = look_up_styles(2)
+        hid1 = hidden(1, frm1, gate1)
+        bands(0, hid0, 4)
+        frm2 = frames(2, bounded2)
+        gate2 = look_up_tones(2)
+        bands(1, hid1, 0)
+        hid2 = hidden(2, frm2, gate2)
+        bands(2, hid2, 2)
+        for q in range(4):
+            nc.sync.dma_start(
+                out_2[0, 4 * q : 4 * q + 4, :].bitcast(I32), out_scales[32 * q : 32 * q + 4, :].bitcast(I32)
+            )

@@ -19,10 +19,11 @@ SIGMOID = mybir.ActivationFunctionType.Sigmoid
 
 P = 128
 PACK = 4
-LIST = 16
+QUADRANTS = 4
+LIST_ROWS = 16
 SPARE = 16
 BANK = 512
-CHUNKS = (512, 256, 256)
+CHUNKS = (256, 512, 256)
 
 
 def tile_picked_yttsfrm_gate_po_kernel(
@@ -34,202 +35,210 @@ def tile_picked_yttsfrm_gate_po_kernel(
         keep = ctx.enter_context(tc.tile_pool(name="keep", bufs=1))
         psum = ctx.enter_context(tc.psum_pool(name="psum", bufs=1))
 
-        def sb(name, shape, dtype):
+        def sbuf(name, shape, dtype):
             return keep.tile(shape, dtype, name=name, align_bytes=64)
 
         def bank(b):
             return psum.tile([P, BANK], F32, name="bank%d" % b)
 
         def load_list(name, src):
-            t = sb(name, list(src.shape), U16)
-            nc.sync.dma_start(t[:], src)
-            return t
+            offsets = sbuf(name, list(src.shape), U16)
+            nc.sync.dma_start(offsets[:], src)
+            return offsets
 
         def load_words(name, words):
-            t = sb(name + "_words", [P, T], U32)
-            nc.sync.dma_start(t[:].bitcast(I32), words[0].rearrange("p n r -> p (n r)").bitcast(I32))
-            return t
+            table = sbuf(name + "_words", [P, T], U32)
+            nc.sync.dma_start(table[:].bitcast(I32), words[0].rearrange("p n r -> p (n r)").bitcast(I32))
+            return table
 
-        def load_scales(name, scales, queue):
-            t = sb(name + "_scales", [P, T], U8)
-            nc.gpsimd.memset(t[:].bitcast(I32), 0)
-            for q in range(4):
-                queue.dma_start(t[32 * q : 32 * q + 4, :].bitcast(I32), scales[0, 4 * q : 4 * q + 4, :].bitcast(I32))
-            return t
+        def load_scales(name, scales):
+            table = sbuf(name + "_scales", [P, T], U8)
+            nc.gpsimd.memset(table[:].bitcast(I32), 0)
+            for q in range(QUADRANTS):
+                nc.sync.dma_start(table[32 * q : 32 * q + 4, :].bitcast(I32), scales[0, 4 * q : 4 * q + 4, :].bitcast(I32))
+            return table
+
+        def load_scales_repeated(name, scales):
+            table = sbuf(name + "_scales", [P, T], U8)
+            for q in range(QUADRANTS):
+                rows = scales[0, 4 * q : 4 * q + 4, :].bitcast(I32)
+                nc.sync.dma_start(
+                    table[32 * q : 32 * q + 32, :].bitcast(I32), rows.unsqueeze(0).to_broadcast([8, 4, T // 4])
+                )
+            return table
 
         def load_weight(name, w, parts):
             width = w.shape[1] // parts
             raws = []
             for h in range(parts):
-                raw = sb("%s_raw%d" % (name, h), [P, PACK, width], F32)
+                raw = sbuf("%s_raw%d" % (name, h), [P, PACK, width], F32)
                 nc.sync.dma_start(raw[:], w[:, h * width : (h + 1) * width].rearrange("(p j) c -> p j c", j=PACK))
                 raws.append(raw)
             return raws
 
-        def pick(name, words, scales, offsets):
-            picked_scales = sb(name + "_picked_scales", [P, S], U8)
-            picked_words = sb(name + "_picked_words", [P, S], U32)
-            nc.vector.tensor_copy(picked_words[:], words[:].indirect(offsets[:]))
-            nc.vector.tensor_copy(picked_scales[:], scales[:].indirect(offsets[:]))
+        def pick(name, word_table, scale_table, offsets):
+            picked_scales = sbuf(name + "_picked_scales", [P, S], U8)
+            picked_words = sbuf(name + "_picked_words", [P, S], U32)
+            nc.vector.tensor_copy(picked_scales[:], scale_table[:].indirect(offsets[:]))
+            nc.vector.tensor_copy(picked_words[:], word_table[:].indirect(offsets[:]))
             return picked_words, picked_scales
 
-        def quantise(name, grouped, width):
-            codes = sb(name + "_codes", [P, width], U32)
-            scales = sb(name + "_qscales", [P, width], U8)
-            nc.vector.quantize_mx(out=codes[:].bitcast(FP8X4), scales=scales[:], in_=grouped)
-            return codes, scales
+        def quantise(name, grouped, width, calls):
+            codes = sbuf(name + "_codes", [P, width], U32)
+            scale_bytes = sbuf(name + "_scale_bytes", [P, width], U8)
+            step = width // calls
+            for h in range(calls):
+                cols = slice(h * step, (h + 1) * step)
+                nc.vector.quantize_mx(
+                    out=codes[:, cols].bitcast(FP8X4), scales=scale_bytes[:, cols],
+                    in_=grouped[:, PACK * h * step : PACK * (h + 1) * step],
+                )
+            return codes, scale_bytes
 
-        def quantise_weight(name, raws, copies):
-            grouped = sb(name + "_bf16", [P, PACK, P, PACK], BF16)
+        def quantise_weight(name, raws, copies, staging, calls):
+            grouped = sbuf(staging, [P, PACK, P, PACK], BF16)
             m = P // len(raws)
             for h in range(len(raws)):
                 copies[h](
-                    grouped[:, :, h * m : (h + 1) * m, :].rearrange("p t m j -> p m j t"),
-                    raws[h][:].rearrange("p j (m t) -> p m j t", t=PACK),
+                    grouped[:, :, h * m : (h + 1) * m, :].rearrange("p (u e) m j -> p u m j e", e=2),
+                    raws[h][:].rearrange("p j (m u e) -> p u m j e", u=2, e=2),
                 )
-            return quantise(name, grouped[:].rearrange("p t m j -> p (t m j)"), PACK * P)
+            return quantise(name, grouped[:].rearrange("p t m j -> p (t m j)"), PACK * P, calls)
 
-        def product(out, weight, t, moving):
+        def product(acc, weight, t, moving):
             cols = slice(t * P, (t + 1) * P)
             nc.tensor.matmul_mx(
-                out=out, lhsT=weight[0][:, cols].bitcast(FP8X4), lhsT_scale=weight[1][:, cols],
+                out=acc, lhsT=weight[0][:, cols].bitcast(FP8X4), lhsT_scale=weight[1][:, cols],
                 rhs=moving[0][:].bitcast(FP8X4), rhs_scale=moving[1][:], start=True, stop=True,
             )
 
-        def window(name):
-            t = sb(name, [P, S + SPARE], F32)
-            nc.gpsimd.memset(t[:, S:], 0.0)
-            return t
-
-        d_scale_table = load_scales("d", d_scales, nc.scalar)
-        sty_l = load_list("sty_l", sty)
+        sty_list = load_list("sty_list", sty)
+        d_scale_table = load_scales_repeated("d", d_scales)
         d_word_table = load_words("d", d_words)
         w3_raw = load_weight("w3", w3, 2)
-        x_scale_table = load_scales("x", x_scales, nc.gpsimd)
-        e_scale_table = load_scales("e", e_scales, nc.gpsimd)
-        offs_l = load_list("offs_l", offs)
-        x_word_table = load_words("x", x_words)
-        mix_l = load_list("mix_l", mix_)
-        w1_raw = load_weight("w1", w1, 1)
-        sp1_l = load_list("sp1_l", sp1)
-        unit_t = sb("unit_t", [P, PACK], F32)
-        nc.sync.dma_start(unit_t[:], unit.rearrange("(p t) o -> p (t o)", t=PACK))
-        ton_l = load_list("ton_l", ton)
+        mix_list = load_list("mix_list", mix_)
+        ton_list = load_list("ton_list", ton)
         e_word_table = load_words("e", e_words)
         w2_raw = load_weight("w2", w2, 1)
-        ph_l = load_list("ph_l", ph)
-        tn_l = load_list("tn_l", tn)
+        offs_list = load_list("offs_list", offs)
+        e_scale_table = load_scales("e", e_scales)
+        x_word_table = load_words("x", x_words)
+        w1_raw = load_weight("w1", w1, 1)
+        x_scale_table = load_scales("x", x_scales)
+        sp1_list = load_list("sp1_list", sp1)
+        tn_list = load_list("tn_list", tn)
+        unit_rows = sbuf("unit_rows", [P, PACK], F32)
+        nc.sync.dma_start(unit_rows[:], unit.rearrange("(p t) o -> p (t o)", t=PACK))
+        ph_list = load_list("ph_list", ph)
         w4_raw = load_weight("w4", w4, 1)
 
-        yd = [window("yd%d" % t) for t in range(PACK)]
-        phoneme = [window("phoneme%d" % t) for t in range(PACK)]
-        tone = [window("tone%d" % t) for t in range(PACK)]
-        style2 = [sb("style2_%d" % t, [P, 2 * S], F32) for t in range(PACK)]
+        yd = [sbuf("yd%d" % t, [P, S + SPARE], F32) for t in range(PACK)]
+        phoneme = [sbuf("phoneme%d" % t, [P, S + SPARE], F32) for t in range(PACK)]
+        tone = [sbuf("tone%d" % t, [P, S + SPARE], F32) for t in range(PACK)]
+        style = [sbuf("style%d" % t, [P, 2 * S], F32) for t in range(PACK)]
+        for t in range(PACK):
+            nc.vector.memset(yd[t][:, S:], 0.0)
+            nc.vector.memset(phoneme[t][:, S:], 0.0)
+            nc.scalar.activation(tone[t][:, S:], yd[t][:, S:], SIGMOID)
 
-        d_picked = pick("d", d_word_table, d_scale_table, sty_l)
-        w3_q = quantise_weight("w3", w3_raw, (nc.scalar.copy, nc.vector.tensor_copy))
+        d_picked = pick("d", d_word_table, d_scale_table, sty_list)
+        w3_q = quantise_weight("w3", w3_raw, (nc.scalar.copy, nc.vector.tensor_copy), "w3_bf16", 2)
         yd_banks = [bank(t) for t in range(PACK)]
         for t in range(PACK):
             product(yd_banks[t][:], w3_q, t, d_picked)
         for t in range(PACK):
             nc.scalar.copy(yd[t][:, :S], yd_banks[t][:])
-            nc.scalar.activation(style2[t][:, S:], yd[t][:].indirect(mix_l[:]), COPY)
+            nc.scalar.activation(style[t][:, S:], yd[t][:].indirect(mix_list[:]), COPY, scale=0.5)
+            nc.gpsimd.tensor_tensor(style[t][:, :S], yd[t][:, :S], style[t][:, S:], ADD)
 
-        x_picked = pick("x", x_word_table, x_scale_table, offs_l)
-        w1_q = quantise_weight("w1", w1_raw, (nc.vector.tensor_copy,))
-        unit2 = sb("unit2", [P, PACK], F32)
-        nc.vector.tensor_scalar(unit2[:], unit_t[:], 2.0, None, MULT)
+        e_picked = pick("e", e_word_table, e_scale_table, ton_list)
+        w2_q = quantise_weight("w2", w2_raw, (nc.vector.tensor_copy,), "w2_bf16", 1)
         for t in range(PACK):
-            nc.vector.scalar_tensor_tensor(style2[t][:, :S], yd_banks[t][:], 2.0, style2[t][:, S:], MULT, ADD)
+            ye_bank = bank(PACK + t)
+            product(ye_bank[:], w2_q, t, e_picked)
+            nc.scalar.activation(tone[t][:, :S], ye_bank[:], SIGMOID)
+
+        x_picked = pick("x", x_word_table, x_scale_table, offs_list)
+        w1_q = quantise_weight("w1", w1_raw, (nc.vector.tensor_copy,), "w1_w4_bf16", 1)
+        unit_twice = sbuf("unit_twice", [P, PACK], F32)
+        nc.vector.tensor_scalar(unit_twice[:], unit_rows[:], 2.0, None, MULT)
         for t in range(PACK):
-            y_bank = bank(PACK + t)
+            y_bank = bank(t)
             product(y_bank[:], w1_q, t, x_picked)
-            nc.scalar.activation(phoneme[t][:, :S], y_bank[:], COPY, scale=unit2[:, t : t + 1])
-
-        e_picked = pick("e", e_word_table, e_scale_table, ton_l)
-        w2_q = quantise_weight("w2", w2_raw, (nc.vector.tensor_copy,))
+            nc.vector.tensor_scalar(phoneme[t][:, :S], y_bank[:], unit_twice[:, t : t + 1], None, MULT)
 
         starts = [sum(CHUNKS[:c]) for c in range(len(CHUNKS))]
 
         def piece(offsets, c):
-            return offsets[:, starts[c] // LIST : (starts[c] + CHUNKS[c]) // LIST]
+            return offsets[:, starts[c] // LIST_ROWS : (starts[c] + CHUNKS[c]) // LIST_ROWS]
 
         def look_up_styles(c):
-            bounded = sb("bounded%d" % c, [P, PACK, CHUNKS[c]], F32)
+            bounded = [sbuf("bounded%d" % t, [P, CHUNKS[c]], F32) for t in range(PACK)]
             for t in range(PACK):
-                nc.scalar.activation(bounded[:, t, :], style2[t][:].indirect(piece(sp1_l, c)), SIGMOID)
+                nc.scalar.activation(bounded[t][:], style[t][:].indirect(piece(sp1_list, c)), SIGMOID, scale=2.0)
             return bounded
 
-        def frames(c, bounded):
-            frm = sb("frm%d" % c, [P, PACK, CHUNKS[c]], F32)
-            for t in range(PACK):
-                nc.vector.tensor_tensor(frm[:, t, :], phoneme[t][:].indirect(piece(ph_l, c)), bounded[:, t, :], MULT)
-            return frm
-
         def look_up_tones(c):
-            gate = sb("gate%d" % c, [P, PACK, CHUNKS[c]], F32)
+            gate = sbuf("gate", [P, PACK, CHUNKS[c]], F32)
             for t in range(PACK):
-                nc.scalar.activation(gate[:, t, :], tone[t][:].indirect(piece(tn_l, c)), COPY)
+                nc.scalar.activation(gate[:, t, :], tone[t][:].indirect(piece(tn_list, c)), COPY)
             return gate
 
-        def by_fours(grouped, planes):
-            return (
-                grouped[:].rearrange("p (c i) t -> p c t i", i=4),
-                [a[:].rearrange("p t (c i) -> p c t i", i=4) for a in planes],
-            )
+        def frames(c, bounded):
+            frm = sbuf("frm", [P, PACK, CHUNKS[c]], F32)
+            for t in range(PACK):
+                nc.vector.tensor_tensor(frm[:, t, :], phoneme[t][:].indirect(piece(ph_list, c)), bounded[t][:], MULT)
+            return frm
+
+        def as_words(grouped):
+            return grouped[:].rearrange("p (c i) t -> p c t i", i=2)
+
+        def as_row_tiles(tiles):
+            return tiles[:].rearrange("p t (c i) -> p c t i", i=2)
 
         def hidden(c, frm, gate):
-            hid = sb("hid%d" % c, [P, CHUNKS[c], PACK], BF16)
-            dst, (a, b) = by_fours(hid, (frm, gate))
-            nc.vector.tensor_tensor(dst, a, b, MULT)
-            return quantise("hid%d" % c, hid[:].rearrange("p n t -> p (n t)"), CHUNKS[c])
+            hid = sbuf("hid%d" % c, [P, CHUNKS[c], PACK], BF16)
+            nc.vector.tensor_tensor(as_words(hid), as_row_tiles(frm), as_row_tiles(gate), MULT)
+            return quantise("hid%d" % c, hid[:].rearrange("p n t -> p (n t)"), CHUNKS[c], 1)
 
-        out_scales = sb("out_scales", [P, U], U8)
+        out_scales = sbuf("out_scales", [P, U], U8)
         out_rows = out_0.rearrange("(p t) r -> p t r", t=PACK)
         out_words = out_1[0].rearrange("p n r -> p (n r)").bitcast(I32)
 
-        def bands(c, hid_q, first_bank):
+        def bands(c, hid_q, w4_q):
             n = CHUNKS[c]
             cols = slice(starts[c], starts[c] + n)
             per_bank = BANK // n
-            result = sb("result%d" % c, [P, PACK, n], F32)
+            first_bank = PACK * ((c + 1) % 2)
+            result = sbuf("result%d" % c, [P, PACK, n], F32)
             for b in range(PACK // per_bank):
                 acc = bank(first_bank + b)
                 for s in range(per_bank):
                     product(acc[:, s * n : (s + 1) * n], w4_q, b * per_bank + s, hid_q)
                 ts = slice(b * per_bank, (b + 1) * per_bank)
                 nc.scalar.copy(result[:, ts, :].rearrange("p t n -> p (t n)"), acc[:])
-            nc.sync.dma_start(out_rows[:, :, cols], result[:])
-            rounded = sb("rounded%d" % c, [P, n, PACK], BF16)
-            dst, (src,) = by_fours(rounded, (result,))
-            nc.vector.tensor_copy(dst, src)
-            codes = sb("out_codes%d" % c, [P, n], U32)
+                nc.sync.dma_start(out_rows[:, ts, cols], result[:, ts, :])
+            rounded = sbuf("rounded%d" % c, [P, n, PACK], BF16)
+            round_copy = nc.scalar.copy if c == 0 else nc.vector.tensor_copy
+            round_copy(as_words(rounded), as_row_tiles(result))
+            out_codes = sbuf("out_codes%d" % c, [P, n], U32)
             nc.vector.quantize_mx(
-                out=codes[:].bitcast(FP8X4), scales=out_scales[:, cols], in_=rounded[:].rearrange("p n t -> p (n t)")
+                out=out_codes[:].bitcast(FP8X4), scales=out_scales[:, cols], in_=rounded[:].rearrange("p n t -> p (n t)")
             )
-            nc.sync.dma_start(out_words[:, cols], codes[:].bitcast(I32))
+            nc.sync.dma_start(out_words[:, cols], out_codes[:].bitcast(I32))
 
-        bounded0 = look_up_styles(0)
-        for t in range(PACK):
-            ye_bank = bank(t)
-            product(ye_bank[:], w2_q, t, e_picked)
-            nc.scalar.activation(tone[t][:, :S], ye_bank[:], SIGMOID)
-        w4_q = quantise_weight("w4", w4_raw, (nc.vector.tensor_copy,))
-        frm0 = frames(0, bounded0)
-        gate0 = look_up_tones(0)
-        bounded1 = look_up_styles(1)
-        hid0 = hidden(0, frm0, gate0)
-        frm1 = frames(1, bounded1)
-        gate1 = look_up_tones(1)
-        bounded2 = look_up_styles(2)
-        hid1 = hidden(1, frm1, gate1)
-        bands(0, hid0, 4)
-        frm2 = frames(2, bounded2)
-        gate2 = look_up_tones(2)
-        bands(1, hid1, 0)
-        hid2 = hidden(2, frm2, gate2)
-        bands(2, hid2, 2)
-        for q in range(4):
-            nc.sync.dma_start(
-                out_2[0, 4 * q : 4 * q + 4, :].bitcast(I32), out_scales[32 * q : 32 * q + 4, :].bitcast(I32)
-            )
+        hid_q = []
+        for c in range(len(CHUNKS)):
+            bounded = look_up_styles(c)
+            gate = look_up_tones(c)
+            frm = frames(c, bounded)
+            if c == 0:
+                w4_q = quantise_weight("w4", w4_raw, (nc.vector.tensor_copy,), "w1_w4_bf16", 1)
+            hid_q.append(hidden(c, frm, gate))
+            if c > 0:
+                bands(c - 1, hid_q[c - 1], w4_q)
+        bands(len(CHUNKS) - 1, hid_q[-1], w4_q)
+
+        for q in range(QUADRANTS):
+            queue = nc.scalar if q % 2 else nc.sync
+            queue.dma_start(out_2[0, 4 * q : 4 * q + 4, :].bitcast(I32), out_scales[32 * q : 32 * q + 4, :].bitcast(I32))

from contextlib import ExitStack

import concourse.mybir as mybir

K, T, S, H, N, U = 512, 1024, 512, 512, 512, 1024
FLOPS = 2 * K * H * S * 3 + 2 * H * N * U

F32 = mybir.dt.float32
BF16 = mybir.dt.bfloat16
I32 = mybir.dt.int32
U32 = mybir.dt.uint32
U16 = mybir.dt.uint16
U8 = mybir.dt.uint8
FP8X4 = mybir.dt.float8_e4m3fn_x4
MULT = mybir.AluOpType.mult
ADD = mybir.AluOpType.add
COPY = mybir.ActivationFunctionType.Copy
SIGMOID = mybir.ActivationFunctionType.Sigmoid

P = 128
PACK = 4
QUADRANTS = 4
LIST_ROWS = 16
SPARE = 16
BANK = 512
CHUNKS = (256, 512, 256)


def tile_picked_yttsfrm_gate_po_kernel(
    tc, x_words, x_scales, w1, e_words, e_scales, w2, d_words, d_scales, w3, unit, w4,
    offs, ton, sty, ph, tn, mix_, sp1, out_0, out_1, out_2,
):
    nc = tc.nc
    with ExitStack() as ctx:
        keep = ctx.enter_context(tc.tile_pool(name="keep", bufs=1))
        psum = ctx.enter_context(tc.psum_pool(name="psum", bufs=1))

        def sbuf(name, shape, dtype):
            return keep.tile(shape, dtype, name=name, align_bytes=64)

        def bank(b):
            return psum.tile([P, BANK], F32, name="bank%d" % b)

        def load_list(name, src):
            offsets = sbuf(name, list(src.shape), U16)
            nc.sync.dma_start(offsets[:], src)
            return offsets

        def load_words(name, words):
            table = sbuf(name + "_words", [P, T], U32)
            nc.sync.dma_start(table[:].bitcast(I32), words[0].rearrange("p n r -> p (n r)").bitcast(I32))
            return table

        def load_scales(name, scales):
            table = sbuf(name + "_scales", [P, T], U8)
            nc.gpsimd.memset(table[:].bitcast(I32), 0)
            for q in range(QUADRANTS):
                nc.sync.dma_start(table[32 * q : 32 * q + 4, :].bitcast(I32), scales[0, 4 * q : 4 * q + 4, :].bitcast(I32))
            return table

        def load_scales_repeated(name, scales):
            table = sbuf(name + "_scales", [P, T], U8)
            for q in range(QUADRANTS):
                rows = scales[0, 4 * q : 4 * q + 4, :].bitcast(I32)
                nc.sync.dma_start(
                    table[32 * q : 32 * q + 32, :].bitcast(I32), rows.unsqueeze(0).to_broadcast([8, 4, T // 4])
                )
            return table

        def load_weight(name, w, parts):
            width = w.shape[1] // parts
            raws = []
            for h in range(parts):
                raw = sbuf("%s_raw%d" % (name, h), [P, PACK, width], F32)
                nc.sync.dma_start(raw[:], w[:, h * width : (h + 1) * width].rearrange("(p j) c -> p j c", j=PACK))
                raws.append(raw)
            return raws

        def pick(name, word_table, scale_table, offsets):
            picked_scales = sbuf(name + "_picked_scales", [P, S], U8)
            picked_words = sbuf(name + "_picked_words", [P, S], U32)
            nc.vector.tensor_copy(picked_scales[:], scale_table[:].indirect(offsets[:]))
            nc.vector.tensor_copy(picked_words[:], word_table[:].indirect(offsets[:]))
            return picked_words, picked_scales

        def quantise(name, grouped, width, calls):
            codes = sbuf(name + "_codes", [P, width], U32)
            scale_bytes = sbuf(name + "_scale_bytes", [P, width], U8)
            step = width // calls
            for h in range(calls):
                cols = slice(h * step, (h + 1) * step)
                nc.vector.quantize_mx(
                    out=codes[:, cols].bitcast(FP8X4), scales=scale_bytes[:, cols],
                    in_=grouped[:, PACK * h * step : PACK * (h + 1) * step],
                )
            return codes, scale_bytes

        def quantise_weight(name, raws, copies, staging, calls):
            grouped = sbuf(staging, [P, PACK, P, PACK], BF16)
            m = P // len(raws)
            for h in range(len(raws)):
                copies[h](
                    grouped[:, :, h * m : (h + 1) * m, :].rearrange("p (u e) m j -> p u m j e", e=2),
                    raws[h][:].rearrange("p j (m u e) -> p u m j e", u=2, e=2),
                )
            return quantise(name, grouped[:].rearrange("p t m j -> p (t m j)"), PACK * P, calls)

        def product(acc, weight, t, moving):
            cols = slice(t * P, (t + 1) * P)
            nc.tensor.matmul_mx(
                out=acc, lhsT=weight[0][:, cols].bitcast(FP8X4), lhsT_scale=weight[1][:, cols],
                rhs=moving[0][:].bitcast(FP8X4), rhs_scale=moving[1][:], start=True, stop=True,
            )

        sty_list = load_list("sty_list", sty)
        d_scale_table = load_scales_repeated("d", d_scales)
        d_word_table = load_words("d", d_words)
        w3_raw = load_weight("w3", w3, 2)
        mix_list = load_list("mix_list", mix_)
        ton_list = load_list("ton_list", ton)
        e_word_table = load_words("e", e_words)
        w2_raw = load_weight("w2", w2, 1)
        offs_list = load_list("offs_list", offs)
        e_scale_table = load_scales("e", e_scales)
        x_word_table = load_words("x", x_words)
        w1_raw = load_weight("w1", w1, 1)
        x_scale_table = load_scales("x", x_scales)
        sp1_list = load_list("sp1_list", sp1)
        tn_list = load_list("tn_list", tn)
        unit_rows = sbuf("unit_rows", [P, PACK], F32)
        nc.sync.dma_start(unit_rows[:], unit.rearrange("(p t) o -> p (t o)", t=PACK))
        ph_list = load_list("ph_list", ph)
        w4_raw = load_weight("w4", w4, 1)

        yd = [sbuf("yd%d" % t, [P, S + SPARE], F32) for t in range(PACK)]
        phoneme = [sbuf("phoneme%d" % t, [P, S + SPARE], F32) for t in range(PACK)]
        tone = [sbuf("tone%d" % t, [P, S + SPARE], F32) for t in range(PACK)]
        style = [sbuf("style%d" % t, [P, 2 * S], F32) for t in range(PACK)]
        for t in range(PACK):
            nc.vector.memset(yd[t][:, S:], 0.0)
            nc.vector.memset(phoneme[t][:, S:], 0.0)
            nc.scalar.activation(tone[t][:, S:], yd[t][:, S:], SIGMOID)

        d_picked = pick("d", d_word_table, d_scale_table, sty_list)
        w3_q = quantise_weight("w3", w3_raw, (nc.scalar.copy, nc.vector.tensor_copy), "w3_bf16", 2)
        yd_banks = [bank(t) for t in range(PACK)]
        for t in range(PACK):
            product(yd_banks[t][:], w3_q, t, d_picked)
        for t in range(PACK):
            nc.scalar.copy(yd[t][:, :S], yd_banks[t][:])
            nc.scalar.activation(style[t][:, S:], yd[t][:].indirect(mix_list[:]), COPY, scale=0.5)
            nc.gpsimd.tensor_tensor(style[t][:, :S], yd[t][:, :S], style[t][:, S:], ADD)

        e_picked = pick("e", e_word_table, e_scale_table, ton_list)
        w2_q = quantise_weight("w2", w2_raw, (nc.vector.tensor_copy,), "w2_bf16", 1)
        for t in range(PACK):
            ye_bank = bank(PACK + t)
            product(ye_bank[:], w2_q, t, e_picked)
            nc.scalar.activation(tone[t][:, :S], ye_bank[:], SIGMOID)

        x_picked = pick("x", x_word_table, x_scale_table, offs_list)
        w1_q = quantise_weight("w1", w1_raw, (nc.vector.tensor_copy,), "w1_w4_bf16", 1)
        unit_twice = sbuf("unit_twice", [P, PACK], F32)
        nc.vector.tensor_scalar(unit_twice[:], unit_rows[:], 2.0, None, MULT)
        for t in range(PACK):
            y_bank = bank(t)
            product(y_bank[:], w1_q, t, x_picked)
            nc.vector.tensor_scalar(phoneme[t][:, :S], y_bank[:], unit_twice[:, t : t + 1], None, MULT)

        starts = [sum(CHUNKS[:c]) for c in range(len(CHUNKS))]

        def piece(offsets, c):
            return offsets[:, starts[c] // LIST_ROWS : (starts[c] + CHUNKS[c]) // LIST_ROWS]

        def look_up_styles(c):
            bounded = [sbuf("bounded%d" % t, [P, CHUNKS[c]], F32) for t in range(PACK)]
            for t in range(PACK):
                nc.scalar.activation(bounded[t][:], style[t][:].indirect(piece(sp1_list, c)), SIGMOID, scale=2.0)
            return bounded

        def look_up_tones(c):
            gate = sbuf("gate", [P, PACK, CHUNKS[c]], F32)
            for t in range(PACK):
                nc.scalar.activation(gate[:, t, :], tone[t][:].indirect(piece(tn_list, c)), COPY)
            return gate

        def frames(c, bounded):
            frm = sbuf("frm", [P, PACK, CHUNKS[c]], F32)
            for t in range(PACK):
                nc.vector.tensor_tensor(frm[:, t, :], phoneme[t][:].indirect(piece(ph_list, c)), bounded[t][:], MULT)
            return frm

        def as_words(grouped):
            return grouped[:].rearrange("p (c i) t -> p c t i", i=2)

        def as_row_tiles(tiles):
            return tiles[:].rearrange("p t (c i) -> p c t i", i=2)

        def hidden(c, frm, gate):
            hid = sbuf("hid%d" % c, [P, CHUNKS[c], PACK], BF16)
            nc.vector.tensor_tensor(as_words(hid), as_row_tiles(frm), as_row_tiles(gate), MULT)
            return quantise("hid%d" % c, hid[:].rearrange("p n t -> p (n t)"), CHUNKS[c], 1)

        out_scales = sbuf("out_scales", [P, U], U8)
        out_rows = out_0.rearrange("(p t) r -> p t r", t=PACK)
        out_words = out_1[0].rearrange("p n r -> p (n r)").bitcast(I32)

        def bands(c, hid_q, w4_q):
            n = CHUNKS[c]
            cols = slice(starts[c], starts[c] + n)
            per_bank = BANK // n
            first_bank = PACK * ((c + 1) % 2)
            result = sbuf("result%d" % c, [P, PACK, n], F32)
            for b in range(PACK // per_bank):
                acc = bank(first_bank + b)
                for s in range(per_bank):
                    product(acc[:, s * n : (s + 1) * n], w4_q, b * per_bank + s, hid_q)
                ts = slice(b * per_bank, (b + 1) * per_bank)
                nc.scalar.copy(result[:, ts, :].rearrange("p t n -> p (t n)"), acc[:])
                nc.sync.dma_start(out_rows[:, ts, cols], result[:, ts, :])
            rounded = sbuf("rounded%d" % c, [P, n, PACK], BF16)
            round_copy = nc.scalar.copy if c == 0 else nc.vector.tensor_copy
            round_copy(as_words(rounded), as_row_tiles(result))
            out_codes = sbuf("out_codes%d" % c, [P, n], U32)
            nc.vector.quantize_mx(
                out=out_codes[:].bitcast(FP8X4), scales=out_scales[:, cols], in_=rounded[:].rearrange("p n t -> p (n t)")
            )
            nc.sync.dma_start(out_words[:, cols], out_codes[:].bitcast(I32))

        hid_q = []
        for c in range(len(CHUNKS)):
            bounded = look_up_styles(c)
            gate = look_up_tones(c)
            frm = frames(c, bounded)
            if c == 0:
                w4_q = quantise_weight("w4", w4_raw, (nc.vector.tensor_copy,), "w1_w4_bf16", 1)
            hid_q.append(hidden(c, frm, gate))
            if c > 0:
                bands(c - 1, hid_q[c - 1], w4_q)
        bands(len(CHUNKS) - 1, hid_q[-1], w4_q)

        for q in range(QUADRANTS):
            queue = nc.scalar if q % 2 else nc.sync
            queue.dma_start(out_2[0, 4 * q : 4 * q + 4, :].bitcast(I32), out_scales[32 * q : 32 * q + 4, :].bitcast(I32))
